import numpy as np
import ml_dtypes


def mxq(x, axis, fmt="e4m3"):
    dtype, down = {"e4m3": (ml_dtypes.float8_e4m3fn, 7), "e5m2": (ml_dtypes.float8_e5m2, 14)}[fmt]
    v = np.moveaxis(np.asarray(x, np.float32).astype(ml_dtypes.bfloat16).astype(np.float64), axis, -1)
    blocks = v.reshape(v.shape[:-1] + (-1, 32))
    amax = np.abs(blocks).max(-1, keepdims=True)
    byte = np.maximum(np.where(amax > 0, np.frexp(amax)[1] - 1 + 127, 0) - down, 1)
    scale = np.exp2(byte - 127.0)
    codes = (blocks / scale).astype(np.float32).astype(dtype).astype(np.float64)
    return np.moveaxis((codes * scale).reshape(v.shape), -1, axis)


WIDE = False


def mx_kscale(k):
    if not WIDE:
        return np.ones(k)
    levels = np.array([30, -30])
    if k % 512:
        return np.exp2(np.random.permutation(np.resize(levels, k // 32))).repeat(32)
    a = np.empty((k // 512, 16))
    for p in range(k // 512):
        a[p, :8] = np.random.permutation(np.resize(levels, 8))
        for g in range(8):
            far = levels[np.abs(levels - a[p, g]) >= 10]
            a[p, g + 8] = far[np.random.randint(len(far))]
    return np.exp2(a.ravel()).repeat(32)


def f64(x):
    return np.asarray(x).astype(np.float64)


def striped(idx):
    return np.tile(np.asarray(idx).reshape(-1, 16).T, (8, 1)).astype(np.uint16)


def unstriped(offs):
    return offs[:16].T.reshape(-1).astype(np.int64)


E2M1 = np.array([0.0, 0.5, 1.0, 1.5, 2.0, 3.0, 4.0, 6.0, -0.0, -0.5, -1.0, -1.5, -2.0, -3.0, -4.0, -6.0])


def pack_weight(w, fmt):
    k, n = w.shape
    w = f64(np.asarray(w, np.float32).astype(ml_dtypes.bfloat16)).reshape(k // 32, 32, n)
    amax = np.abs(w).max(1)
    if fmt in ("e4m3", "e5m2"):
        byte = np.frexp(amax)[1] - 1 + 127 - (7 if fmt == "e4m3" else 14)
    else:
        mant, ex = np.frexp(amax / 6.0)
        byte = np.where(mant > 0.5, ex, ex - 1) + 127
    byte = np.clip(np.where(amax > 0, byte, 1), 1, 254)
    scaled = (w * np.exp2(127.0 - byte)[:, None, :]).reshape(k, n).astype(np.float32)
    by_word = np.ascontiguousarray(scaled.reshape(k // 512, 128, 4, n).transpose(0, 1, 3, 2))
    if fmt in ("e4m3", "e5m2"):
        words = by_word.astype(ml_dtypes.float8_e4m3fn if fmt == "e4m3" else ml_dtypes.float8_e5m2).view(np.uint8)
    else:
        c = by_word.astype(ml_dtypes.float4_e2m1fn).view(np.uint8) & 0xF
        words = (c[..., 0::2] | (c[..., 1::2] << 4)).reshape(k // 512, 128, 2 * n)
    return np.ascontiguousarray(words), np.ascontiguousarray(byte.astype(np.uint8).reshape(k // 512, 16, n))


def unpack_weight(words, scales, fmt):
    g, _, n = scales.shape
    words = np.ascontiguousarray(words).reshape(g, 128, n, -1)
    if fmt in ("e4m3", "e5m2"):
        vals = words.view(ml_dtypes.float8_e4m3fn if fmt == "e4m3" else ml_dtypes.float8_e5m2).astype(np.float64)
    else:
        nib = np.empty((g, 128, n, 4), np.uint8)
        nib[..., 0::2] = words & 0xF
        nib[..., 1::2] = words >> 4
        vals = E2M1[nib]
    vals = vals * np.repeat(np.exp2(scales.astype(np.float64) - 127.0), 8, axis=1)[..., None]
    return vals.transpose(0, 1, 3, 2).reshape(g * 512, n)


def sigmoid(v):
    return 1.0 / (1.0 + np.exp(-v))


K, T, J, R, O, N, L, E = 512, 2048, 256, 512, 128, 256, 512, 512


def setup_inputs():
    n = np.random.standard_normal
    idx = np.random.permutation(T)[:J]
    idx2 = np.random.permutation(T)[:J]
    idx3 = np.random.permutation(T)[:J]
    idx4 = np.random.permutation(J)[:O]
    idx5 = np.random.permutation(J)[:O]
    idx6 = np.random.permutation(E)[:O]
    fk = mx_kscale(K)
    fr = mx_kscale(R)
    fl = mx_kscale(L)
    xtp = pack_weight(n((K, T)) / fk[:, None], "e4m3")
    wp = pack_weight(n((K, R)) * 1 / np.sqrt(K) * fk[:, None] * fr, "e2m1")
    wbp = pack_weight(n((R, N)) * 1 / np.sqrt(R) / fr[:, None], "e5m2")
    sxp = pack_weight(n((L, O)) / fl[:, None], "e2m1")
    wsp = pack_weight(n((L, N)) * 1 / np.sqrt(L) * fl[:, None], "e5m2")
    return {
        "xt_words": xtp[0],
        "xt_scales": xtp[1],
        "w_words": wp[0],
        "w_scales": wp[1],
        "wb_words": wbp[0],
        "wb_scales": wbp[1],
        "sx_words": sxp[0],
        "sx_scales": sxp[1],
        "ws_words": wsp[0],
        "ws_scales": wsp[1],
        "tz": (n((N, E))).astype(np.float32),
        "so": (np.random.uniform(0.6, 1.6, (N, 1))).astype(np.float32),
        "bo": (np.random.uniform(-1.0, 1.0, (N, 1))).astype(np.float32),
        "offs": striped(idx),
        "offs2": striped(idx2),
        "offs3": striped(idx3),
        "offs4": striped(idx4),
        "offs5": striped(idx5),
        "offs6": striped(idx6),
    }


def reference(xt_words, xt_scales, w_words, w_scales, wb_words, wb_scales, sx_words, sx_scales, ws_words, ws_scales, tz, so, bo, offs, offs2, offs3, offs4, offs5, offs6):
    idx = unstriped(offs)
    idx2 = unstriped(offs2)
    idx3 = unstriped(offs3)
    idx4 = unstriped(offs4)
    idx5 = unstriped(offs5)
    idx6 = unstriped(offs6)
    xtu = unpack_weight(xt_words, xt_scales, "e4m3")
    wu = unpack_weight(w_words, w_scales, "e2m1")
    wbu = unpack_weight(wb_words, wb_scales, "e5m2")
    sxu = unpack_weight(sx_words, sx_scales, "e2m1")
    wsu = unpack_weight(ws_words, ws_scales, "e5m2")
    xtidxg = xtu[:, idx]
    a = wu.T @ xtidxg
    xtidx2g = xtu[:, idx2]
    b = wu.T @ xtidx2g
    xtidx3g = xtu[:, idx3]
    g0 = wu.T @ xtidx3g
    c1 = np.maximum(b, g0)
    hid = np.abs(a[:, idx4] - c1[:, idx5])
    hidq = mxq(hid, 0, "e4m3")
    p = wbu.T @ hidq + wsu.T @ sxu
    y = p * sigmoid(f64(tz)[:, idx6] * f64(so) + f64(bo))
    return y

@@ -1,0 +1,211 @@
+from contextlib import ExitStack
+
+import concourse.mybir as mybir
+
+K, T, J, R, O, N, L, E = 512, 2048, 256, 512, 128, 256, 512, 512
+FLOPS = 2 * (3 * K * R * J + R * N * O + L * N * O)
+
+F32 = mybir.dt.float32
+BF16 = mybir.dt.bfloat16
+I32 = mybir.dt.int32
+U32 = mybir.dt.uint32
+U16 = mybir.dt.uint16
+U8 = mybir.dt.uint8
+E4M3 = mybir.dt.float8_e4m3fn_x4
+E5M2 = mybir.dt.float8_e5m2_x4
+E2M1 = mybir.dt.float4_e2m1fn_x4
+ALU = mybir.AluOpType
+ACT = mybir.ActivationFunctionType
+
+P = 128
+PACK = 4
+HALVES = N // P
+
+
+def load_scale_rows(queue, plane, scales):
+    for q in range(4):
+        queue.dma_start(out=plane[32 * q : 32 * q + 4, :].bitcast(I32), in_=scales[0, 4 * q : 4 * q + 4, :].bitcast(I32))
+
+
+def load_scale_quadrant(queue, plane, scales, q):
+    queue.dma_start(out=plane[32 * q : 32 * q + 4, :].bitcast(I32), in_=scales[0, 4 * q : 4 * q + 4, :].bitcast(I32))
+
+
+def tile_list_triple_looked_skip_finalgate_kernel(
+    tc, xt_words, xt_scales, w_words, w_scales, wb_words, wb_scales, sx_words, sx_scales, ws_words, ws_scales,
+    tz, so, bo, offs, offs2, offs3, offs4, offs5, offs6, out,
+):
+    nc = tc.nc
+    with ExitStack() as ctx:
+        keep = ctx.enter_context(tc.tile_pool(name="keep", bufs=1))
+        psum = ctx.enter_context(tc.psum_pool(name="psum", bufs=8))
+
+        def held(shape, dtype, name, tag=None):
+            return keep.tile(shape, dtype, name=name, tag=tag or name, align_bytes=64)
+
+        list_a = held([P, J // 16], U16, "list_a")
+        list_b = held([P, J // 16], U16, "list_b")
+        list_g = held([P, J // 16], U16, "list_g")
+        pick_a = held([P, O // 16], U16, "pick_a")
+        pick_c = held([P, O // 16], U16, "pick_c")
+        pick_z = held([P, O // 16], U16, "pick_z")
+        xt_w = held([P, T], U32, "xt_w")
+        xt_s = held([P, T], U8, "xt_s")
+        w_w = held([P, 2 * R], U8, "w_w")
+        w_s = held([P, R], U8, "w_s", "reused")
+        wb_w = held([P, N], U32, "wb_w")
+        wb_s = held([P, N], U8, "wb_s")
+        ws_w = held([P, N], U32, "ws_w")
+        ws_s = held([P, N], U8, "ws_s")
+        sx_w = held([P, 2 * O], U8, "sx_w")
+        sx_s = held([P, O], U8, "sx_s")
+        tz_rows = [held([P, E], F32, f"tz_rows{h}") for h in range(HALVES)]
+        slope = held([P, HALVES], F32, "slope")
+        offset = held([P, HALVES], F32, "offset")
+
+        nc.gpsimd.memset(xt_s[:, 0:1280].bitcast(I32), 0)
+        nc.vector.memset(xt_s[:, 1280:T].bitcast(I32), 0)
+        for plane in (w_s, wb_s, ws_s, sx_s):
+            nc.vector.memset(plane[:].bitcast(I32), 0)
+
+        nc.sync.dma_start(list_a[:], offs)
+        nc.sync.dma_start(list_g[:], offs3)
+        nc.sync.dma_start(list_b[:], offs2)
+        load_scale_quadrant(nc.scalar, xt_s, xt_scales, 0)
+        load_scale_quadrant(nc.sync, xt_s, xt_scales, 2)
+        load_scale_quadrant(nc.scalar, xt_s, xt_scales, 1)
+        load_scale_quadrant(nc.sync, xt_s, xt_scales, 3)
+        nc.sync.dma_start(out=xt_w[:].bitcast(I32), in_=xt_words[0].rearrange("p n t -> p (n t)").bitcast(I32))
+        load_scale_rows(nc.sync, w_s, w_scales)
+        nc.sync.dma_start(out=w_w[:].bitcast(I32), in_=w_words[0].bitcast(I32))
+        nc.sync.dma_start(pick_a[:], offs4)
+        nc.sync.dma_start(out=tz_rows[0][:], in_=tz[0:P, :])
+        nc.sync.dma_start(pick_c[:], offs5)
+        nc.sync.dma_start(pick_z[:], offs6)
+        with nc.allow_non_contiguous_dma(reason="one value for each output feature, features on the partitions"):
+            nc.sync.dma_start(out=slope[:], in_=so.rearrange("(h p) o -> p (h o)", p=P))
+            nc.sync.dma_start(out=offset[:], in_=bo.rearrange("(h p) o -> p (h o)", p=P))
+        load_scale_rows(nc.sync, ws_s, ws_scales)
+        nc.sync.dma_start(out=tz_rows[1][:], in_=tz[P : 2 * P, :])
+        nc.sync.dma_start(out=ws_w[:].bitcast(I32), in_=ws_words[0].rearrange("p n t -> p (n t)").bitcast(I32))
+        nc.sync.dma_start(out=sx_w[:].bitcast(I32), in_=sx_words[0].bitcast(I32))
+        nc.sync.dma_start(out=wb_w[:].bitcast(I32), in_=wb_words[0].rearrange("p n t -> p (n t)").bitcast(I32))
+        for q in range(4):
+            load_scale_quadrant(nc.gpsimd if q < 2 else nc.sync, sx_s, sx_scales, q)
+        load_scale_rows(nc.sync, wb_s, wb_scales)
+
+        def gather_scales(offsets, name):
+            got = held([P, J], U8, name)
+            nc.vector.tensor_copy(got[:], xt_s[:].indirect(offsets[:]))
+            return got
+
+        xa_s = gather_scales(list_a, "xa_s")
+        xg_s = gather_scales(list_g, "xg_s")
+        xb_s = gather_scales(list_b, "xb_s")
+        xa_w = held([P, J], U32, "xa_w")
+        nc.vector.tensor_copy(xa_w[:], xt_w[:].indirect(list_a[:]))
+        w_dealt = held([P, 2 * R], U8, "w_dealt")
+        w_dealt_s = held([P, R], U8, "w_dealt_s")
+        for u in range(2):
+            nc.scalar.copy(
+                w_dealt[:].bitcast(U16).rearrange("p (t m) -> p m t", t=PACK)[:, :, 2 * u : 2 * u + 2],
+                w_w[:].bitcast(U16).rearrange("p (m t) -> p m t", t=PACK)[:, :, 2 * u : 2 * u + 2],
+            )
+        nc.vector.tensor_copy(
+            w_dealt_s[:].rearrange("p (t m) -> p m t", t=PACK),
+            w_s[:].rearrange("p (m t) -> p m t", t=PACK),
+        )
+        xgb_w = held([P, 2 * J], U32, "xgb_w", "reused")
+        xg_w, xb_w = xgb_w[:, 0:J], xgb_w[:, J : 2 * J]
+        nc.vector.tensor_copy(xg_w, xt_w[:].indirect(list_g[:]))
+        nc.vector.tensor_copy(xb_w, xt_w[:].indirect(list_b[:]))
+
+        def first_product(t, words, scales):
+            acc = psum.tile([P, J], F32, name="acc")
+            nc.tensor.matmul_mx(
+                out=acc[:],
+                lhsT=w_dealt[:, 2 * P * t : 2 * P * (t + 1)].bitcast(E2M1),
+                lhsT_scale=w_dealt_s[:, P * t : P * (t + 1)],
+                rhs=words.bitcast(E4M3),
+                rhs_scale=scales[:],
+                start=True,
+                stop=True,
+            )
+            return acc
+
+        a_picked = held([P, PACK, O], F32, "a_picked")
+        diff = held([P, PACK, O], F32, "diff", "diff_then_gate")
+        hid = held([P, O, PACK], BF16, "hid")
+
+        def to_sbuf(acc, name):
+            rows = held([P, J], F32, name)
+            nc.scalar.copy(rows[:], acc[:])
+            return rows
+
+        def product_a(t):
+            return to_sbuf(first_product(t, xa_w[:], xa_s), f"a_rows{t}")
+
+        def product_g(t):
+            return to_sbuf(first_product(t, xg_w, xg_s), f"g_rows{t}")
+
+        def larger(t, g_rows):
+            b_acc = first_product(t, xb_w, xb_s)
+            c_rows = held([P, J], F32, f"c_rows{t}")
+            nc.vector.tensor_tensor(c_rows[:], b_acc[:], g_rows[:], ALU.max)
+            return c_rows
+
+        def difference(t, c_rows):
+            nc.vector.tensor_tensor(diff[:, t, :], c_rows[:].indirect(pick_c[:]), a_picked[:, t, :], ALU.subtract)
+
+        for t in range(2):
+            nc.vector.tensor_copy(a_picked[:, t, :], product_a(t)[:].indirect(pick_a[:]))
+        g_first = [product_g(t) for t in range(2)]
+        c_first = [larger(t, g_first[t]) for t in range(2)]
+        for t in range(2):
+            difference(t, c_first[t])
+        c_last = []
+        for t in range(2, PACK):
+            a_rows = product_a(t)
+            g_rows = product_g(t)
+            nc.scalar.activation(out=a_picked[:, t, :], in_=a_rows[:].indirect(pick_a[:]), func=ACT.Copy)
+            c_last.append(larger(t, g_rows))
+        for t in range(2, PACK):
+            difference(t, c_last[t - 2])
+        for u in range(2):
+            nc.scalar.activation(
+                out=hid[:, :, 2 * u : 2 * u + 2],
+                in_=diff[:, 2 * u : 2 * u + 2, :].rearrange("p t o -> p o t"),
+                func=ACT.Abs,
+            )
+
+        gates = []
+        for h, follows in enumerate(("a_rows3", "diff_then_gate")):
+            gate = held([P, O], F32, f"gate{h}", follows)
+            nc.scalar.activation(
+                out=gate[:], in_=tz_rows[h][:].indirect(pick_z[:]), func=ACT.Sigmoid,
+                bias=offset[:, h : h + 1], scale=slope[:, h : h + 1],
+            )
+            gates.append(gate)
+
+        hid_w = held([P, O], U32, "hid_w")
+        hid_s = held([P, O], U8, "hid_s")
+        nc.vector.quantize_mx(out=hid_w[:].bitcast(E4M3), scales=hid_s[:], in_=hid[:].rearrange("p o t -> p (o t)"))
+
+        result = held([P, HALVES, O], F32, "result")
+        sums = []
+        for h in range(HALVES):
+            acc = psum.tile([P, J], F32, name="acc")
+            cols = slice(P * h, P * (h + 1))
+            nc.tensor.matmul_mx(
+                out=acc[:, 0:O], lhsT=ws_w[:, cols].bitcast(E5M2), lhsT_scale=ws_s[:, cols],
+                rhs=sx_w[:].bitcast(E2M1), rhs_scale=sx_s[:], start=True, stop=False,
+            )
+            sums.append(acc)
+        for h in range(HALVES):
+            cols = slice(P * h, P * (h + 1))
+            nc.tensor.matmul_mx(
+                out=sums[h][:, 0:O], lhsT=wb_w[:, cols].bitcast(E5M2), lhsT_scale=wb_s[:, cols],
+                rhs=hid_w[:].bitcast(E4M3), rhs_scale=hid_s[:], start=False, stop=True,
+            )
+            nc.vector.tensor_tensor(result[:, h, :], sums[h][:, 0:O], gates[h][:], ALU.mult)
+        nc.sync.dma_start(out=out.rearrange("(h p) o -> p h o", p=P), in_=result[:])

@@ -94,6 +94,11 @@ def tile_list_triple_looked_skip_finalgate_kernel(
             load_scale_quadrant(nc.gpsimd if q < 2 else nc.sync, sx_s, sx_scales, q)
         load_scale_rows(nc.sync, wb_s, wb_scales)
 
+        warm = held([P, 1], F32, "warm")
+        warm_out = held([P, 1], F32, "warm_out")
+        nc.vector.memset(warm[:], 0.0)
+        nc.scalar.activation(out=warm_out[:], in_=warm[:], func=ACT.Sigmoid)
+
         def gather_scales(offsets, name):
             got = held([P, J], U8, name)
             nc.vector.tensor_copy(got[:], xt_s[:].indirect(offsets[:]))

@@ -63,9 +63,7 @@ def tile_list_triple_looked_skip_finalgate_kernel(
         slope = held([P, HALVES], F32, "slope")
         offset = held([P, HALVES], F32, "offset")
 
-        nc.gpsimd.memset(xt_s[:, 0:1280].bitcast(I32), 0)
-        nc.vector.memset(xt_s[:, 1280:T].bitcast(I32), 0)
-        for plane in (w_s, wb_s, ws_s, sx_s):
+        for plane in (xt_s, w_s, wb_s, ws_s, sx_s):
             nc.vector.memset(plane[:].bitcast(I32), 0)
 
         nc.sync.dma_start(list_a[:], offs)
@@ -91,7 +89,7 @@ def tile_list_triple_looked_skip_finalgate_kernel(
         nc.sync.dma_start(out=sx_w[:].bitcast(I32), in_=sx_words[0].bitcast(I32))
         nc.sync.dma_start(out=wb_w[:].bitcast(I32), in_=wb_words[0].rearrange("p n t -> p (n t)").bitcast(I32))
         for q in range(4):
-            load_scale_quadrant(nc.gpsimd if q < 2 else nc.sync, sx_s, sx_scales, q)
+            load_scale_quadrant(nc.gpsimd if q < 3 else nc.sync, sx_s, sx_scales, q)
         load_scale_rows(nc.sync, wb_s, wb_scales)
 
         warm = held([P, 1], F32, "warm")
@@ -116,10 +114,10 @@ def tile_list_triple_looked_skip_finalgate_kernel(
                 w_dealt[:].bitcast(U16).rearrange("p (t m) -> p m t", t=PACK)[:, :, 2 * u : 2 * u + 2],
                 w_w[:].bitcast(U16).rearrange("p (m t) -> p m t", t=PACK)[:, :, 2 * u : 2 * u + 2],
             )
-        nc.vector.tensor_copy(
-            w_dealt_s[:].rearrange("p (t m) -> p m t", t=PACK),
-            w_s[:].rearrange("p (m t) -> p m t", t=PACK),
-        )
+            nc.vector.tensor_copy(
+                w_dealt_s[:].rearrange("p (t m) -> p m t", t=PACK)[:, :, 2 * u : 2 * u + 2],
+                w_s[:].rearrange("p (m t) -> p m t", t=PACK)[:, :, 2 * u : 2 * u + 2],
+            )
         xgb_w = held([P, 2 * J], U32, "xgb_w", "reused")
         xg_w, xb_w = xgb_w[:, 0:J], xgb_w[:, J : 2 * J]
         nc.vector.tensor_copy(xg_w, xt_w[:].indirect(list_g[:]))
@@ -162,20 +160,25 @@ def tile_list_triple_looked_skip_finalgate_kernel(
         def difference(t, c_rows):
             nc.vector.tensor_tensor(diff[:, t, :], c_rows[:].indirect(pick_c[:]), a_picked[:, t, :], ALU.subtract)
 
+        def pick_on_vector(t, rows):
+            nc.vector.tensor_copy(a_picked[:, t, :], rows[:].indirect(pick_a[:]))
+
+        def pick_on_scalar(t, rows):
+            nc.scalar.activation(out=a_picked[:, t, :], in_=rows[:].indirect(pick_a[:]), func=ACT.Copy)
+
+        a_rows = [product_a(t) for t in range(3)]
         for t in range(2):
-            nc.vector.tensor_copy(a_picked[:, t, :], product_a(t)[:].indirect(pick_a[:]))
-        g_first = [product_g(t) for t in range(2)]
-        c_first = [larger(t, g_first[t]) for t in range(2)]
-        for t in range(2):
-            difference(t, c_first[t])
-        c_last = []
+            pick_on_vector(t, a_rows[t])
+        difference(0, larger(0, product_g(0)))
+        a_rows.append(product_a(3))
+        c1 = larger(1, product_g(1))
+        c2 = larger(2, product_g(2))
+        difference(1, c1)
+        c3 = larger(3, product_g(3))
         for t in range(2, PACK):
-            a_rows = product_a(t)
-            g_rows = product_g(t)
-            nc.scalar.activation(out=a_picked[:, t, :], in_=a_rows[:].indirect(pick_a[:]), func=ACT.Copy)
-            c_last.append(larger(t, g_rows))
-        for t in range(2, PACK):
-            difference(t, c_last[t - 2])
+            pick_on_scalar(t, a_rows[t])
+        difference(2, c2)
+        difference(3, c3)
         for u in range(2):
             nc.scalar.activation(
                 out=hid[:, :, 2 * u : 2 * u + 2],

@@ -88,8 +88,7 @@ def tile_list_triple_looked_skip_finalgate_kernel(
         nc.sync.dma_start(out=ws_w[:].bitcast(I32), in_=ws_words[0].rearrange("p n t -> p (n t)").bitcast(I32))
         nc.sync.dma_start(out=sx_w[:].bitcast(I32), in_=sx_words[0].bitcast(I32))
         nc.sync.dma_start(out=wb_w[:].bitcast(I32), in_=wb_words[0].rearrange("p n t -> p (n t)").bitcast(I32))
-        for q in range(4):
-            load_scale_quadrant(nc.gpsimd if q < 3 else nc.sync, sx_s, sx_scales, q)
+        load_scale_rows(nc.gpsimd, sx_s, sx_scales)
         load_scale_rows(nc.sync, wb_s, wb_scales)
 
         warm = held([P, 1], F32, "warm")

from contextlib import ExitStack

import concourse.mybir as mybir

K, T, J, R, O, N, L, E = 512, 2048, 256, 512, 128, 256, 512, 512
FLOPS = 2 * (3 * K * R * J + R * N * O + L * N * O)

F32 = mybir.dt.float32
BF16 = mybir.dt.bfloat16
I32 = mybir.dt.int32
U32 = mybir.dt.uint32
U16 = mybir.dt.uint16
U8 = mybir.dt.uint8
E4M3 = mybir.dt.float8_e4m3fn_x4
E5M2 = mybir.dt.float8_e5m2_x4
E2M1 = mybir.dt.float4_e2m1fn_x4
ALU = mybir.AluOpType
ACT = mybir.ActivationFunctionType

P = 128
PACK = 4
HALVES = N // P


def load_scale_rows(queue, plane, scales):
    for q in range(4):
        queue.dma_start(out=plane[32 * q : 32 * q + 4, :].bitcast(I32), in_=scales[0, 4 * q : 4 * q + 4, :].bitcast(I32))


def load_scale_quadrant(queue, plane, scales, q):
    queue.dma_start(out=plane[32 * q : 32 * q + 4, :].bitcast(I32), in_=scales[0, 4 * q : 4 * q + 4, :].bitcast(I32))


def tile_list_triple_looked_skip_finalgate_kernel(
    tc, xt_words, xt_scales, w_words, w_scales, wb_words, wb_scales, sx_words, sx_scales, ws_words, ws_scales,
    tz, so, bo, offs, offs2, offs3, offs4, offs5, offs6, out,
):
    nc = tc.nc
    with ExitStack() as ctx:
        keep = ctx.enter_context(tc.tile_pool(name="keep", bufs=1))
        psum = ctx.enter_context(tc.psum_pool(name="psum", bufs=8))

        def held(shape, dtype, name, tag=None):
            return keep.tile(shape, dtype, name=name, tag=tag or name, align_bytes=64)

        list_a = held([P, J // 16], U16, "list_a")
        list_b = held([P, J // 16], U16, "list_b")
        list_g = held([P, J // 16], U16, "list_g")
        pick_a = held([P, O // 16], U16, "pick_a")
        pick_c = held([P, O // 16], U16, "pick_c")
        pick_z = held([P, O // 16], U16, "pick_z")
        xt_w = held([P, T], U32, "xt_w")
        xt_s = held([P, T], U8, "xt_s")
        w_w = held([P, 2 * R], U8, "w_w")
        w_s = held([P, R], U8, "w_s", "reused")
        wb_w = held([P, N], U32, "wb_w")
        wb_s = held([P, N], U8, "wb_s")
        ws_w = held([P, N], U32, "ws_w")
        ws_s = held([P, N], U8, "ws_s")
        sx_w = held([P, 2 * O], U8, "sx_w")
        sx_s = held([P, O], U8, "sx_s")
        tz_rows = [held([P, E], F32, f"tz_rows{h}") for h in range(HALVES)]
        slope = held([P, HALVES], F32, "slope")
        offset = held([P, HALVES], F32, "offset")

        for plane in (xt_s, w_s, wb_s, ws_s, sx_s):
            nc.vector.memset(plane[:].bitcast(I32), 0)

        nc.sync.dma_start(list_a[:], offs)
        nc.sync.dma_start(list_g[:], offs3)
        nc.sync.dma_start(list_b[:], offs2)
        load_scale_quadrant(nc.scalar, xt_s, xt_scales, 0)
        load_scale_quadrant(nc.sync, xt_s, xt_scales, 2)
        load_scale_quadrant(nc.scalar, xt_s, xt_scales, 1)
        load_scale_quadrant(nc.sync, xt_s, xt_scales, 3)
        nc.sync.dma_start(out=xt_w[:].bitcast(I32), in_=xt_words[0].rearrange("p n t -> p (n t)").bitcast(I32))
        load_scale_rows(nc.sync, w_s, w_scales)
        nc.sync.dma_start(out=w_w[:].bitcast(I32), in_=w_words[0].bitcast(I32))
        nc.sync.dma_start(pick_a[:], offs4)
        nc.sync.dma_start(out=tz_rows[0][:], in_=tz[0:P, :])
        nc.sync.dma_start(pick_c[:], offs5)
        nc.sync.dma_start(pick_z[:], offs6)
        with nc.allow_non_contiguous_dma(reason="one value for each output feature, features on the partitions"):
            nc.sync.dma_start(out=slope[:], in_=so.rearrange("(h p) o -> p (h o)", p=P))
            nc.sync.dma_start(out=offset[:], in_=bo.rearrange("(h p) o -> p (h o)", p=P))
        load_scale_rows(nc.sync, ws_s, ws_scales)
        nc.sync.dma_start(out=tz_rows[1][:], in_=tz[P : 2 * P, :])
        nc.sync.dma_start(out=ws_w[:].bitcast(I32), in_=ws_words[0].rearrange("p n t -> p (n t)").bitcast(I32))
        nc.sync.dma_start(out=sx_w[:].bitcast(I32), in_=sx_words[0].bitcast(I32))
        nc.sync.dma_start(out=wb_w[:].bitcast(I32), in_=wb_words[0].rearrange("p n t -> p (n t)").bitcast(I32))
        load_scale_rows(nc.gpsimd, sx_s, sx_scales)
        load_scale_rows(nc.sync, wb_s, wb_scales)

        warm = held([P, 1], F32, "warm")
        warm_out = held([P, 1], F32, "warm_out")
        nc.vector.memset(warm[:], 0.0)
        nc.scalar.activation(out=warm_out[:], in_=warm[:], func=ACT.Sigmoid)

        def gather_scales(offsets, name):
            got = held([P, J], U8, name)
            nc.vector.tensor_copy(got[:], xt_s[:].indirect(offsets[:]))
            return got

        xa_s = gather_scales(list_a, "xa_s")
        xg_s = gather_scales(list_g, "xg_s")
        xb_s = gather_scales(list_b, "xb_s")
        xa_w = held([P, J], U32, "xa_w")
        nc.vector.tensor_copy(xa_w[:], xt_w[:].indirect(list_a[:]))
        w_dealt = held([P, 2 * R], U8, "w_dealt")
        w_dealt_s = held([P, R], U8, "w_dealt_s")
        for u in range(2):
            nc.scalar.copy(
                w_dealt[:].bitcast(U16).rearrange("p (t m) -> p m t", t=PACK)[:, :, 2 * u : 2 * u + 2],
                w_w[:].bitcast(U16).rearrange("p (m t) -> p m t", t=PACK)[:, :, 2 * u : 2 * u + 2],
            )
            nc.vector.tensor_copy(
                w_dealt_s[:].rearrange("p (t m) -> p m t", t=PACK)[:, :, 2 * u : 2 * u + 2],
                w_s[:].rearrange("p (m t) -> p m t", t=PACK)[:, :, 2 * u : 2 * u + 2],
            )
        xgb_w = held([P, 2 * J], U32, "xgb_w", "reused")
        xg_w, xb_w = xgb_w[:, 0:J], xgb_w[:, J : 2 * J]
        nc.vector.tensor_copy(xg_w, xt_w[:].indirect(list_g[:]))
        nc.vector.tensor_copy(xb_w, xt_w[:].indirect(list_b[:]))

        def first_product(t, words, scales):
            acc = psum.tile([P, J], F32, name="acc")
            nc.tensor.matmul_mx(
                out=acc[:],
                lhsT=w_dealt[:, 2 * P * t : 2 * P * (t + 1)].bitcast(E2M1),
                lhsT_scale=w_dealt_s[:, P * t : P * (t + 1)],
                rhs=words.bitcast(E4M3),
                rhs_scale=scales[:],
                start=True,
                stop=True,
            )
            return acc

        a_picked = held([P, PACK, O], F32, "a_picked")
        diff = held([P, PACK, O], F32, "diff", "diff_then_gate")
        hid = held([P, O, PACK], BF16, "hid")

        def to_sbuf(acc, name):
            rows = held([P, J], F32, name)
            nc.scalar.copy(rows[:], acc[:])
            return rows

        def product_a(t):
            return to_sbuf(first_product(t, xa_w[:], xa_s), f"a_rows{t}")

        def product_g(t):
            return to_sbuf(first_product(t, xg_w, xg_s), f"g_rows{t}")

        def larger(t, g_rows):
            b_acc = first_product(t, xb_w, xb_s)
            c_rows = held([P, J], F32, f"c_rows{t}")
            nc.vector.tensor_tensor(c_rows[:], b_acc[:], g_rows[:], ALU.max)
            return c_rows

        def difference(t, c_rows):
            nc.vector.tensor_tensor(diff[:, t, :], c_rows[:].indirect(pick_c[:]), a_picked[:, t, :], ALU.subtract)

        def pick_on_vector(t, rows):
            nc.vector.tensor_copy(a_picked[:, t, :], rows[:].indirect(pick_a[:]))

        def pick_on_scalar(t, rows):
            nc.scalar.activation(out=a_picked[:, t, :], in_=rows[:].indirect(pick_a[:]), func=ACT.Copy)

        a_rows = [product_a(t) for t in range(3)]
        for t in range(2):
            pick_on_vector(t, a_rows[t])
        difference(0, larger(0, product_g(0)))
        a_rows.append(product_a(3))
        c1 = larger(1, product_g(1))
        c2 = larger(2, product_g(2))
        difference(1, c1)
        c3 = larger(3, product_g(3))
        for t in range(2, PACK):
            pick_on_scalar(t, a_rows[t])
        difference(2, c2)
        difference(3, c3)
        for u in range(2):
            nc.scalar.activation(
                out=hid[:, :, 2 * u : 2 * u + 2],
                in_=diff[:, 2 * u : 2 * u + 2, :].rearrange("p t o -> p o t"),
                func=ACT.Abs,
            )

        gates = []
        for h, follows in enumerate(("a_rows3", "diff_then_gate")):
            gate = held([P, O], F32, f"gate{h}", follows)
            nc.scalar.activation(
                out=gate[:], in_=tz_rows[h][:].indirect(pick_z[:]), func=ACT.Sigmoid,
                bias=offset[:, h : h + 1], scale=slope[:, h : h + 1],
            )
            gates.append(gate)

        hid_w = held([P, O], U32, "hid_w")
        hid_s = held([P, O], U8, "hid_s")
        nc.vector.quantize_mx(out=hid_w[:].bitcast(E4M3), scales=hid_s[:], in_=hid[:].rearrange("p o t -> p (o t)"))

        result = held([P, HALVES, O], F32, "result")
        sums = []
        for h in range(HALVES):
            acc = psum.tile([P, J], F32, name="acc")
            cols = slice(P * h, P * (h + 1))
            nc.tensor.matmul_mx(
                out=acc[:, 0:O], lhsT=ws_w[:, cols].bitcast(E5M2), lhsT_scale=ws_s[:, cols],
                rhs=sx_w[:].bitcast(E2M1), rhs_scale=sx_s[:], start=True, stop=False,
            )
            sums.append(acc)
        for h in range(HALVES):
            cols = slice(P * h, P * (h + 1))
            nc.tensor.matmul_mx(
                out=sums[h][:, 0:O], lhsT=wb_w[:, cols].bitcast(E5M2), lhsT_scale=wb_s[:, cols],
                rhs=hid_w[:].bitcast(E4M3), rhs_scale=hid_s[:], start=False, stop=True,
            )
            nc.vector.tensor_tensor(result[:, h, :], sums[h][:, 0:O], gates[h][:], ALU.mult)
        nc.sync.dma_start(out=out.rearrange("(h p) o -> p h o", p=P), in_=result[:])
